import numpy as np
import ml_dtypes


def mxq(x, axis, fmt="e4m3"):
    dtype, down = {"e4m3": (ml_dtypes.float8_e4m3fn, 7), "e5m2": (ml_dtypes.float8_e5m2, 14)}[fmt]
    v = np.moveaxis(np.asarray(x, np.float32).astype(ml_dtypes.bfloat16).astype(np.float64), axis, -1)
    blocks = v.reshape(v.shape[:-1] + (-1, 32))
    amax = np.abs(blocks).max(-1, keepdims=True)
    byte = np.maximum(np.where(amax > 0, np.frexp(amax)[1] - 1 + 127, 0) - down, 1)
    scale = np.exp2(byte - 127.0)
    codes = (blocks / scale).astype(np.float32).astype(dtype).astype(np.float64)
    return np.moveaxis((codes * scale).reshape(v.shape), -1, axis)


WIDE = False


def mx_kscale(k):
    if not WIDE:
        return np.ones(k)
    levels = np.array([30, -30])
    if k % 512:
        return np.exp2(np.random.permutation(np.resize(levels, k // 32))).repeat(32)
    a = np.empty((k // 512, 16))
    for p in range(k // 512):
        a[p, :8] = np.random.permutation(np.resize(levels, 8))
        for g in range(8):
            far = levels[np.abs(levels - a[p, g]) >= 10]
            a[p, g + 8] = far[np.random.randint(len(far))]
    return np.exp2(a.ravel()).repeat(32)


def f64(x):
    return np.asarray(x).astype(np.float64)


def striped(idx):
    return np.tile(np.asarray(idx).reshape(-1, 16).T, (8, 1)).astype(np.uint16)


def unstriped(offs):
    return offs[:16].T.reshape(-1).astype(np.int64)


K, J, N, T, B, V = 256, 1024, 256, 2048, 128, 2048


def setup_inputs():
    n = np.random.standard_normal
    idx = np.random.permutation(T)[:J]
    idx2 = np.random.permutation(V)[:J]
    fj = mx_kscale(J)
    return {
        "xf": (n((K, T))).astype(np.float32),
        "ra": (np.random.uniform(0.5, 1.5, (1, J)) * fj).astype(np.float32),
        "gt": (n((N, V)) * np.exp(0.5 * n((1, V)))).astype(np.float32),
        "rb": (np.random.uniform(0.5, 1.5, (1, J)) / fj).astype(np.float32),
        "pr": (n((N, J))).astype(np.float32),
        "mom": (1.0 * n((K, N))).astype(np.float32),
        "old": (1.0 * n((K, N))).astype(np.float32),
        "offs": striped(idx),
        "offs2": striped(idx2),
    }


def reference(xf, ra, gt, rb, pr, mom, old, offs, offs2):
    idx = unstriped(offs)
    idx2 = unstriped(offs2)
    xg = f64(xf)[:, idx]
    g1 = xg.reshape(K, B, J // B).mean(axis=2)
    g2 = np.repeat(g1, J // B, axis=1)
    us = (xg - g2) * f64(ra)
    uj = us.T
    gs = (f64(gt)[:, idx2] - f64(pr)) * f64(rb)
    gj = gs.T
    ujq = mxq(uj, 0, "e4m3")
    gjq = mxq(gj, 0, "e5m2")
    w = ujq.T @ gjq
    u2 = 0.04 * w + 0.6 * f64(mom)
    y = f64(old) * 0.5 - u2 / (1.0 + np.abs(u2))
    return y

@@ -1,0 +1,207 @@
+from contextlib import ExitStack
+
+import concourse.mybir as mybir
+from concourse.masks import make_identity
+
+K, J, N, T = 256, 1024, 256, 2048
+FLOPS = 2 * K * J * N
+
+F32 = mybir.dt.float32
+BF16 = mybir.dt.bfloat16
+U32 = mybir.dt.uint32
+U16 = mybir.dt.uint16
+U8 = mybir.dt.uint8
+E4M3X4 = mybir.dt.float8_e4m3fn_x4
+E5M2X4 = mybir.dt.float8_e5m2_x4
+ALU = mybir.AluOpType
+ACT = mybir.ActivationFunctionType
+
+P = 128
+PACK = 4
+PASS = P * PACK
+PASSES = J // PASS
+GROUP = 8
+LIST_COLS = PASS // 16
+HALVES = 2
+
+
+def tile_list_moment_centred_errors_momentum_kernel(tc, xf, ra, gt, rb, pr, mom, old, offs, offs2, out):
+    nc = tc.nc
+    with ExitStack() as ctx:
+        lists = ctx.enter_context(tc.tile_pool(name="lists", bufs=1))
+        keep = ctx.enter_context(tc.tile_pool(name="keep", bufs=1))
+        turn_banks = ctx.enter_context(tc.psum_pool(name="turn_banks", bufs=6))
+        sum_banks = ctx.enter_context(tc.psum_pool(name="sum_banks", bufs=2))
+
+        x_list = lists.tile([P, J // 16], U16, name="x_list")
+        g_list = lists.tile([P, J // 16], U16, name="g_list")
+        x_table = [keep.tile([P, T], F32, name=f"x_table{a}") for a in range(HALVES)]
+        g_table = [keep.tile([P, T], F32, name=f"g_table{h}") for h in range(HALVES)]
+        pred = [[keep.tile([P, PASS], F32, name=f"pred{h}{g}") for g in range(PASSES)] for h in range(HALVES)]
+        ra_t = keep.tile([P, PASSES, PACK], F32, name="ra_t")
+        rb_t = keep.tile([P, PASSES, PACK], F32, name="rb_t")
+        mom_t = keep.tile([P, HALVES, N], F32, name="mom_t")
+        old_t = keep.tile([P, HALVES, N], F32, name="old_t")
+        ident = keep.tile([P, P], F32, name="ident")
+
+        xf_rows = xf.rearrange("(p a) t -> a p t", a=HALVES)
+        nc.sync.dma_start(x_list[:], offs)
+        nc.sync.dma_start(x_table[0][:], xf_rows[0])
+        nc.scalar.dma_start(ra_t[:], ra[0].rearrange("(g p t) -> p g t", g=PASSES, t=PACK))
+        nc.scalar.dma_start(rb_t[:], rb[0].rearrange("(g p t) -> p g t", g=PASSES, t=PACK))
+        nc.sync.dma_start(x_table[1][:], xf_rows[1])
+        nc.sync.dma_start(g_list[:], offs2)
+        for h in range(HALVES):
+            nc.sync.dma_start(g_table[h][:], gt[h * P : (h + 1) * P, :])
+            for g in range(PASSES):
+                nc.sync.dma_start(pred[h][g][:], pr[h * P : (h + 1) * P, g * PASS : (g + 1) * PASS])
+        nc.sync.dma_start(mom_t[:], mom.rearrange("(p a) n -> p a n", a=HALVES))
+        nc.sync.dma_start(old_t[:], old.rearrange("(p a) n -> p a n", a=HALVES))
+        make_identity(nc, ident[:])
+        warm_in = keep.tile([P, 1], F32, name="warm_in")
+        warm_out = keep.tile([P, 1], F32, name="warm_out")
+        nc.vector.memset(warm_in[:], 1.0)
+        nc.scalar.activation(warm_out[:], warm_in[:], ACT.Abs_reciprocal_sqrt, bias=1.0)
+
+        def gather(table, offsets, g, name, on_vector):
+            picked = keep.tile([P, PASS], F32, name=name)
+            window = table[:].indirect(offsets[:, g * LIST_COLS : (g + 1) * LIST_COLS])
+            if on_vector:
+                nc.vector.tensor_copy(picked[:], window)
+            else:
+                nc.scalar.activation(picked[:], window, ACT.Copy)
+            return picked
+
+        def weigh(bank, weights, g, staged):
+            nc.vector.tensor_tensor(
+                staged.rearrange("p (c t) -> p c t", t=PACK),
+                bank[:].rearrange("p t c -> p c t"),
+                weights[:, g, :].unsqueeze(1).to_broadcast([P, P, PACK]),
+                ALU.mult,
+            )
+
+        def centre_and_turn(picked, name):
+            sums = keep.tile([P, PASS // GROUP], F32, name=name + "_sums")
+            nc.vector.tensor_reduce(
+                sums[:], picked[:].rearrange("k (b e) -> k b e", e=GROUP), mybir.AxisListType.X, ALU.add
+            )
+            minus_mean = keep.tile([P, PASS // GROUP, 2], F32, name=name + "_minus_mean")
+            nc.vector.tensor_scalar(
+                minus_mean[:],
+                sums[:].unsqueeze(2).to_broadcast([P, PASS // GROUP, 2]),
+                -1.0 / GROUP,
+                None,
+                ALU.mult,
+            )
+            bank = turn_banks.tile([P, PACK, P], F32, name="turned")
+            for t in range(PACK):
+                nc.tensor.matmul(
+                    bank[:, t, :], picked[:, t::PACK], ident[:], start=(t == 0), stop=False, is_transpose=True
+                )
+            for t in range(PACK):
+                nc.tensor.matmul(
+                    bank[:, t, :],
+                    minus_mean[:].rearrange("k b e -> k (b e)"),
+                    ident[:],
+                    start=False,
+                    stop=(t == PACK - 1),
+                    is_transpose=True,
+                )
+            return bank
+
+        def subtract_and_turn(picked, predicted, name):
+            error = keep.tile([P, PACK, P], F32, name=name)
+            nc.vector.tensor_tensor(
+                error[:].rearrange("n t (q i) -> n q t i", i=4),
+                picked[:].rearrange("n (q i t) -> n q t i", i=4, t=PACK),
+                predicted[:].rearrange("n (q i t) -> n q t i", i=4, t=PACK),
+                ALU.subtract,
+            )
+            bank = turn_banks.tile([P, PACK, P], F32, name="turned")
+            for t in range(PACK):
+                nc.tensor.transpose(bank[:, t, :], error[:, t, :], ident[:])
+            return bank
+
+        u_codes, u_scales = [], []
+        for a in range(HALVES):
+            staged = keep.tile([P, PASSES * PASS], BF16, name=f"u_staged{a}", align_bytes=64)
+            picked = [gather(x_table[a], x_list, g, f"x_picked{a}{g}", a == 0 and g == 1) for g in range(PASSES)]
+            banks = [centre_and_turn(picked[g], f"x{a}{g}") for g in range(PASSES)]
+            for g in range(PASSES):
+                weigh(banks[g], ra_t, g, staged[:, g * PASS : (g + 1) * PASS])
+            codes = keep.tile([P, PASSES * P], U32, name=f"u_codes{a}", align_bytes=64)
+            scales = keep.tile([P, PASSES * P], U8, name=f"u_scales{a}", align_bytes=64)
+            nc.vector.quantize_mx(codes[:].bitcast(E4M3X4), scales[:], staged[:])
+            u_codes.append(codes)
+            u_scales.append(scales)
+
+        out_rows = out.rearrange("(p a) n -> p a n", a=HALVES)
+
+        def multiply(h, g, bank, moment):
+            staged = keep.tile([P, PASS], BF16, name=f"g_staged{h}{g}", align_bytes=64)
+            weigh(bank, rb_t, g, staged[:])
+            codes = keep.tile([P, P], U32, name=f"g_codes{h}{g}", align_bytes=64)
+            scales = keep.tile([P, P], U8, name=f"g_scales{h}{g}", align_bytes=64)
+            nc.vector.quantize_mx(codes[:].bitcast(E5M2X4), scales[:], staged[:])
+            for a in range(HALVES):
+                nc.tensor.matmul_mx(
+                    moment[:, a, :],
+                    lhsT=u_codes[a][:, g * P : (g + 1) * P].bitcast(E4M3X4),
+                    lhsT_scale=u_scales[a][:, g * P : (g + 1) * P],
+                    rhs=codes[:].bitcast(E5M2X4),
+                    rhs_scale=scales[:],
+                    start=(g == 0 and a == 0),
+                    stop=(g == PASSES - 1 and a == HALVES - 1),
+                )
+
+        def finish(h, moment, parts):
+            cols = slice(h * P, (h + 1) * P)
+            tiles = {}
+            for part in parts:
+                rows = part.stop - part.start
+                for what in ("step", "size", "root", "damp", "soft", "result"):
+                    tiles[what, part.start] = keep.tile([P, rows, P], F32, name=f"{what}{h}{part.start}")
+            for part in parts:
+                nc.vector.scalar_tensor_tensor(
+                    tiles["step", part.start][:], mom_t[:, part, cols], 15.0, moment[:, part, :], ALU.mult, ALU.add
+                )
+            for part in parts:
+                nc.scalar.activation(tiles["size", part.start][:], tiles["step", part.start][:], ACT.Abs, scale=0.04)
+            for part in parts:
+                nc.scalar.activation(
+                    tiles["root", part.start][:], tiles["size", part.start][:], ACT.Abs_reciprocal_sqrt, bias=1.0
+                )
+            for part in parts:
+                nc.scalar.activation(tiles["damp", part.start][:], tiles["root", part.start][:], ACT.Square)
+            for part in parts:
+                nc.vector.scalar_tensor_tensor(
+                    tiles["soft", part.start][:],
+                    tiles["step", part.start][:],
+                    0.04,
+                    tiles["damp", part.start][:],
+                    ALU.mult,
+                    ALU.mult,
+                )
+            for part in parts:
+                nc.vector.scalar_tensor_tensor(
+                    tiles["result", part.start][:],
+                    old_t[:, part, cols],
+                    0.5,
+                    tiles["soft", part.start][:],
+                    ALU.mult,
+                    ALU.subtract,
+                )
+                nc.sync.dma_start(out_rows[:, part, cols], tiles["result", part.start][:])
+
+        g_picked = [
+            [gather(g_table[h], g_list, g, f"g_picked{h}{g}", False) for g in range(PASSES)] for h in range(HALVES)
+        ]
+        moments = []
+        for h in range(HALVES):
+            banks = [subtract_and_turn(g_picked[h][g], pred[h][g], f"error{h}{g}") for g in range(PASSES)]
+            moment = sum_banks.tile([P, HALVES, P], F32, name="moment")
+            for g in range(PASSES):
+                multiply(h, g, banks[g], moment)
+            moments.append(moment)
+        finish(0, moments[0], [slice(0, 2)])
+        finish(1, moments[1], [slice(0, 1), slice(1, 2)])

@@ -58,10 +58,6 @@ def tile_list_moment_centred_errors_momentum_kernel(tc, xf, ra, gt, rb, pr, mom,
         nc.sync.dma_start(mom_t[:], mom.rearrange("(p a) n -> p a n", a=HALVES))
         nc.sync.dma_start(old_t[:], old.rearrange("(p a) n -> p a n", a=HALVES))
         make_identity(nc, ident[:])
-        warm_in = keep.tile([P, 1], F32, name="warm_in")
-        warm_out = keep.tile([P, 1], F32, name="warm_out")
-        nc.vector.memset(warm_in[:], 1.0)
-        nc.scalar.activation(warm_out[:], warm_in[:], ACT.Abs_reciprocal_sqrt, bias=1.0)
 
         def gather(table, offsets, g, name, on_vector):
             picked = keep.tile([P, PASS], F32, name=name)

@@ -58,17 +58,67 @@ def tile_list_moment_centred_errors_momentum_kernel(tc, xf, ra, gt, rb, pr, mom,
         nc.sync.dma_start(mom_t[:], mom.rearrange("(p a) n -> p a n", a=HALVES))
         nc.sync.dma_start(old_t[:], old.rearrange("(p a) n -> p a n", a=HALVES))
         make_identity(nc, ident[:])
+        warm_in = keep.tile([P, 1], F32, name="warm_in")
+        warm_out = keep.tile([P, 1], F32, name="warm_out")
+        nc.vector.memset(warm_in[:], 1.0)
+        nc.scalar.activation(warm_out[:], warm_in[:], ACT.Abs_reciprocal_sqrt, bias=1.0)
 
-        def gather(table, offsets, g, name, on_vector):
-            picked = keep.tile([P, PASS], F32, name=name)
-            window = table[:].indirect(offsets[:, g * LIST_COLS : (g + 1) * LIST_COLS])
-            if on_vector:
-                nc.vector.tensor_copy(picked[:], window)
-            else:
-                nc.scalar.activation(picked[:], window, ACT.Copy)
+        def window(table, offsets, g):
+            return table[:].indirect(offsets[:, g * LIST_COLS : (g + 1) * LIST_COLS])
+
+        def gather(table, offsets, g, name):
+            picked = keep.tile([P, PASS], F32, name=name, align_bytes=64)
+            nc.scalar.activation(picked[:], window(table, offsets, g), ACT.Copy)
             return picked
 
-        def weigh(bank, weights, g, staged):
+        def group_means(groups, axis, name):
+            sums = keep.tile([P, PASS // GROUP], F32, name=name + "_sums", align_bytes=64)
+            nc.vector.tensor_reduce(sums[:], groups, axis, ALU.add)
+            minus_mean = keep.tile([P, P], F32, name=name + "_minus_mean")
+            nc.gpsimd.tensor_scalar(
+                minus_mean[:].rearrange("k (b e) -> k b e", e=2),
+                sums[:].unsqueeze(2).to_broadcast([P, PASS // GROUP, 2]),
+                -1.0 / GROUP,
+                0.0,
+                ALU.mult,
+                ALU.add,
+            )
+            return minus_mean
+
+        def means_in_list_order(picked, name):
+            return group_means(picked[:].rearrange("k (b e) -> k b e", e=GROUP), mybir.AxisListType.X, name)
+
+        def turn_adding(slots, minus_mean):
+            bank = turn_banks.tile([P, PACK, P], F32, name="turned")
+            for t in range(PACK):
+                nc.tensor.matmul(bank[:, t, :], slots[t], ident[:], start=(t == 0), stop=False, is_transpose=True)
+            for t in range(PACK):
+                nc.tensor.matmul(
+                    bank[:, t, :], minus_mean[:], ident[:], start=False, stop=(t == PACK - 1), is_transpose=True
+                )
+            return bank
+
+        def stepped(picked):
+            return [picked[:, t::PACK] for t in range(PACK)]
+
+        def combine_and_turn(picked, other, op, name):
+            planes = keep.tile([P, PACK, P], F32, name=name)
+            nc.vector.tensor_tensor(
+                planes[:].rearrange("n t p -> n p t"), picked[:].rearrange("n (p t) -> n p t", t=PACK), other, op
+            )
+            bank = turn_banks.tile([P, PACK, P], F32, name="turned")
+            for t in range(PACK):
+                nc.tensor.transpose(bank[:, t, :], planes[:, t, :], ident[:])
+            return bank
+
+        def error_turned(h, g):
+            predicted = pred[h][g][:].rearrange("n (p t) -> n p t", t=PACK)
+            return combine_and_turn(g_picked[h, g], predicted, ALU.subtract, f"error{h}{g}")
+
+        def staging(passes, name, tag=None):
+            return keep.tile([P, passes * PASS], BF16, name=name, tag=tag or name, align_bytes=64)
+
+        def weigh(staged, bank, weights, g):
             nc.vector.tensor_tensor(
                 staged.rearrange("p (c t) -> p c t", t=PACK),
                 bank[:].rearrange("p t c -> p c t"),
@@ -76,128 +126,102 @@ def tile_list_moment_centred_errors_momentum_kernel(tc, xf, ra, gt, rb, pr, mom,
                 ALU.mult,
             )
 
-        def centre_and_turn(picked, name):
-            sums = keep.tile([P, PASS // GROUP], F32, name=name + "_sums")
-            nc.vector.tensor_reduce(
-                sums[:], picked[:].rearrange("k (b e) -> k b e", e=GROUP), mybir.AxisListType.X, ALU.add
-            )
-            minus_mean = keep.tile([P, PASS // GROUP, 2], F32, name=name + "_minus_mean")
-            nc.vector.tensor_scalar(
-                minus_mean[:],
-                sums[:].unsqueeze(2).to_broadcast([P, PASS // GROUP, 2]),
-                -1.0 / GROUP,
-                None,
-                ALU.mult,
-            )
+        def quantise(staged, fmt, name):
+            words = staged.shape[1] // PACK
+            codes = keep.tile([P, words], U32, name=name + "_codes", align_bytes=64)
+            scales = keep.tile([P, words], U8, name=name + "_scales", align_bytes=64)
+            nc.vector.quantize_mx(codes[:].bitcast(fmt), scales[:], staged[:])
+            return [(codes[:, c : c + P].bitcast(fmt), scales[:, c : c + P]) for c in range(0, words, P)]
+
+        def error_turned_stepped(h, g, engine):
+            error = keep.tile([P, PASS], F32, name=f"error{h}{g}")
+            engine.tensor_tensor(error[:], g_picked[h, g][:], pred[h][g][:], ALU.subtract)
             bank = turn_banks.tile([P, PACK, P], F32, name="turned")
             for t in range(PACK):
-                nc.tensor.matmul(
-                    bank[:, t, :], picked[:, t::PACK], ident[:], start=(t == 0), stop=False, is_transpose=True
-                )
-            for t in range(PACK):
-                nc.tensor.matmul(
-                    bank[:, t, :],
-                    minus_mean[:].rearrange("k b e -> k (b e)"),
-                    ident[:],
-                    start=False,
-                    stop=(t == PACK - 1),
-                    is_transpose=True,
-                )
+                nc.tensor.transpose(bank[:, t, :], error[:, t::PACK], ident[:])
             return bank
 
-        def subtract_and_turn(picked, predicted, name):
-            error = keep.tile([P, PACK, P], F32, name=name)
-            nc.vector.tensor_tensor(
-                error[:].rearrange("n t (q i) -> n q t i", i=4),
-                picked[:].rearrange("n (q i t) -> n q t i", i=4, t=PACK),
-                predicted[:].rearrange("n (q i t) -> n q t i", i=4, t=PACK),
-                ALU.subtract,
-            )
-            bank = turn_banks.tile([P, PACK, P], F32, name="turned")
-            for t in range(PACK):
-                nc.tensor.transpose(bank[:, t, :], error[:, t, :], ident[:])
-            return bank
-
-        u_codes, u_scales = [], []
-        for a in range(HALVES):
-            staged = keep.tile([P, PASSES * PASS], BF16, name=f"u_staged{a}", align_bytes=64)
-            picked = [gather(x_table[a], x_list, g, f"x_picked{a}{g}", a == 0 and g == 1) for g in range(PASSES)]
-            banks = [centre_and_turn(picked[g], f"x{a}{g}") for g in range(PASSES)]
-            for g in range(PASSES):
-                weigh(banks[g], ra_t, g, staged[:, g * PASS : (g + 1) * PASS])
-            codes = keep.tile([P, PASSES * P], U32, name=f"u_codes{a}", align_bytes=64)
-            scales = keep.tile([P, PASSES * P], U8, name=f"u_scales{a}", align_bytes=64)
-            nc.vector.quantize_mx(codes[:].bitcast(E4M3X4), scales[:], staged[:])
-            u_codes.append(codes)
-            u_scales.append(scales)
-
-        out_rows = out.rearrange("(p a) n -> p a n", a=HALVES)
-
-        def multiply(h, g, bank, moment):
-            staged = keep.tile([P, PASS], BF16, name=f"g_staged{h}{g}", align_bytes=64)
-            weigh(bank, rb_t, g, staged[:])
-            codes = keep.tile([P, P], U32, name=f"g_codes{h}{g}", align_bytes=64)
-            scales = keep.tile([P, P], U8, name=f"g_scales{h}{g}", align_bytes=64)
-            nc.vector.quantize_mx(codes[:].bitcast(E5M2X4), scales[:], staged[:])
+        def multiply(moment, h, g):
             for a in range(HALVES):
                 nc.tensor.matmul_mx(
                     moment[:, a, :],
-                    lhsT=u_codes[a][:, g * P : (g + 1) * P].bitcast(E4M3X4),
-                    lhsT_scale=u_scales[a][:, g * P : (g + 1) * P],
-                    rhs=codes[:].bitcast(E5M2X4),
-                    rhs_scale=scales[:],
+                    lhsT=u_q[a, g][0],
+                    lhsT_scale=u_q[a, g][1],
+                    rhs=g_q[h, g][0],
+                    rhs_scale=g_q[h, g][1],
                     start=(g == 0 and a == 0),
                     stop=(g == PASSES - 1 and a == HALVES - 1),
                 )
 
-        def finish(h, moment, parts):
-            cols = slice(h * P, (h + 1) * P)
-            tiles = {}
-            for part in parts:
-                rows = part.stop - part.start
-                for what in ("step", "size", "root", "damp", "soft", "result"):
-                    tiles[what, part.start] = keep.tile([P, rows, P], F32, name=f"{what}{h}{part.start}")
-            for part in parts:
-                nc.vector.scalar_tensor_tensor(
-                    tiles["step", part.start][:], mom_t[:, part, cols], 15.0, moment[:, part, :], ALU.mult, ALU.add
-                )
-            for part in parts:
-                nc.scalar.activation(tiles["size", part.start][:], tiles["step", part.start][:], ACT.Abs, scale=0.04)
-            for part in parts:
-                nc.scalar.activation(
-                    tiles["root", part.start][:], tiles["size", part.start][:], ACT.Abs_reciprocal_sqrt, bias=1.0
-                )
-            for part in parts:
-                nc.scalar.activation(tiles["damp", part.start][:], tiles["root", part.start][:], ACT.Square)
-            for part in parts:
-                nc.vector.scalar_tensor_tensor(
-                    tiles["soft", part.start][:],
-                    tiles["step", part.start][:],
-                    0.04,
-                    tiles["damp", part.start][:],
-                    ALU.mult,
-                    ALU.mult,
-                )
-            for part in parts:
-                nc.vector.scalar_tensor_tensor(
-                    tiles["result", part.start][:],
-                    old_t[:, part, cols],
-                    0.5,
-                    tiles["soft", part.start][:],
-                    ALU.mult,
-                    ALU.subtract,
-                )
-                nc.sync.dma_start(out_rows[:, part, cols], tiles["result", part.start][:])
+        out_rows = out.rearrange("(p a) n -> p a n", a=HALVES)
 
-        g_picked = [
-            [gather(g_table[h], g_list, g, f"g_picked{h}{g}", False) for g in range(PASSES)] for h in range(HALVES)
-        ]
-        moments = []
+        def soften(h, moment, part, tag=None):
+            cols = slice(h * P, (h + 1) * P)
+            shape = [P, part.stop - part.start, P]
+            name = f"{h}{part.start}"
+            step = keep.tile(shape, F32, name="step" + name, tag=tag or "step" + name, align_bytes=64)
+            nc.vector.scalar_tensor_tensor(step[:], mom_t[:, part, cols], 15.0, moment[:, part, :], ALU.mult, ALU.add)
+            size = keep.tile(shape, F32, name="size" + name)
+            nc.scalar.activation(size[:], step[:], ACT.Abs, scale=0.04)
+            root = keep.tile(shape, F32, name="root" + name)
+            nc.scalar.activation(root[:], size[:], ACT.Abs_reciprocal_sqrt, bias=1.0)
+            damp = keep.tile(shape, F32, name="damp" + name)
+            nc.scalar.activation(damp[:], root[:], ACT.Square)
+            return step, damp
+
+        def finish(h, part, step, damp):
+            cols = slice(h * P, (h + 1) * P)
+            shape = [P, part.stop - part.start, P]
+            name = f"{h}{part.start}"
+            soft = keep.tile(shape, F32, name="soft" + name)
+            nc.vector.scalar_tensor_tensor(soft[:], step[:], 0.04, damp[:], ALU.mult, ALU.mult)
+            result = keep.tile(shape, F32, name="result" + name)
+            nc.vector.scalar_tensor_tensor(result[:], old_t[:, part, cols], 0.5, soft[:], ALU.mult, ALU.subtract)
+            nc.sync.dma_start(out_rows[:, part, cols], result[:])
+
+        u_q, g_q, g_picked = {}, {}, {}
+        x00 = gather(x_table[0], x_list, 0, "x_picked00")
+        x01 = keep.tile([P, PACK, P], F32, name="x_picked01")
+        nc.vector.tensor_copy(x01[:].rearrange("k t p -> k p t"), window(x_table[0], x_list, 1))
+        m01 = group_means(x01[:].rearrange("k t (b e) -> k b t e", e=2), mybir.AxisListType.XY, "x01")
+        m00 = means_in_list_order(x00, "x00")
+        b01 = turn_adding([x01[:, t, :] for t in range(PACK)], m01)
+        b00 = turn_adding(stepped(x00), m00)
+        x1 = [gather(x_table[1], x_list, g, f"x_picked1{g}") for g in range(PASSES)]
         for h in range(HALVES):
-            banks = [subtract_and_turn(g_picked[h][g], pred[h][g], f"error{h}{g}") for g in range(PASSES)]
-            moment = sum_banks.tile([P, HALVES, P], F32, name="moment")
             for g in range(PASSES):
-                multiply(h, g, banks[g], moment)
-            moments.append(moment)
-        finish(0, moments[0], [slice(0, 2)])
-        finish(1, moments[1], [slice(0, 1), slice(1, 2)])
+                g_picked[h, g] = gather(g_table[h], g_list, g, f"g_picked{h}{g}")
+        m1 = [means_in_list_order(x1[g], f"x1{g}") for g in range(PASSES)]
+        b1 = [turn_adding(stepped(x1[g]), m1[g]) for g in range(PASSES)]
+        su = staging(4, "u_staged", tag="x10_sums")
+        weigh(su[:, PASS : 2 * PASS], b01, ra_t, 1)
+        weigh(su[:, :PASS], b00, ra_t, 0)
+        weigh(su[:, 2 * PASS : 3 * PASS], b1[0], ra_t, 0)
+        weigh(su[:, 3 * PASS :], b1[1], ra_t, 1)
+        e00 = error_turned_stepped(0, 0, nc.gpsimd)
+        e01 = error_turned_stepped(0, 1, nc.gpsimd)
+        u_q[0, 0], u_q[0, 1], u_q[1, 0], u_q[1, 1] = quantise(su, E4M3X4, "u")
+        e10 = error_turned_stepped(1, 0, nc.vector)
+        t0 = staging(2, "g_staged0", tag="g_picked10")
+        weigh(t0[:, :PASS], e00, rb_t, 0)
+        e11 = error_turned_stepped(1, 1, nc.vector)
+        weigh(t0[:, PASS:], e01, rb_t, 1)
+        t10 = staging(1, "g_staged10")
+        weigh(t10[:], e10, rb_t, 0)
+        g_q[0, 0], g_q[0, 1] = quantise(t0, E5M2X4, "g0")
+        t11 = staging(1, "g_staged11")
+        weigh(t11[:], e11, rb_t, 1)
+        moments = [sum_banks.tile([P, HALVES, P], F32, name="moment") for h in range(HALVES)]
+        multiply(moments[0], 0, 0)
+        multiply(moments[0], 0, 1)
+        (g_q[1, 0],) = quantise(t10, E5M2X4, "g10")
+        (g_q[1, 1],) = quantise(t11, E5M2X4, "g11")
+        whole = slice(0, HALVES)
+        first = soften(0, moments[0], whole)
+        multiply(moments[1], 1, 0)
+        multiply(moments[1], 1, 1)
+        parts = [slice(a, a + 1) for a in range(HALVES)]
+        last = [soften(1, moments[1], part) for part in parts]
+        finish(0, whole, *first)
+        for part, pair in zip(parts, last):
+            finish(1, part, *pair)

@@ -30,8 +30,8 @@ def tile_list_moment_centred_errors_momentum_kernel(tc, xf, ra, gt, rb, pr, mom,
     with ExitStack() as ctx:
         lists = ctx.enter_context(tc.tile_pool(name="lists", bufs=1))
         keep = ctx.enter_context(tc.tile_pool(name="keep", bufs=1))
-        turn_banks = ctx.enter_context(tc.psum_pool(name="turn_banks", bufs=6))
-        sum_banks = ctx.enter_context(tc.psum_pool(name="sum_banks", bufs=2))
+        turn_banks = ctx.enter_context(tc.psum_pool(name="turn_banks", bufs=5))
+        sum_banks = ctx.enter_context(tc.psum_pool(name="sum_banks", bufs=1))
 
         x_list = lists.tile([P, J // 16], U16, name="x_list")
         g_list = lists.tile([P, J // 16], U16, name="g_list")
@@ -45,16 +45,22 @@ def tile_list_moment_centred_errors_momentum_kernel(tc, xf, ra, gt, rb, pr, mom,
         ident = keep.tile([P, P], F32, name="ident")
 
         xf_rows = xf.rearrange("(p a) t -> a p t", a=HALVES)
-        nc.sync.dma_start(x_list[:], offs)
+
+        def load_predictions(h, g):
+            nc.sync.dma_start(pred[h][g][:], pr[h * P : (h + 1) * P, g * PASS : (g + 1) * PASS])
+
         nc.sync.dma_start(x_table[0][:], xf_rows[0])
-        nc.scalar.dma_start(ra_t[:], ra[0].rearrange("(g p t) -> p g t", g=PASSES, t=PACK))
-        nc.scalar.dma_start(rb_t[:], rb[0].rearrange("(g p t) -> p g t", g=PASSES, t=PACK))
+        nc.sync.dma_start(x_list[:], offs)
         nc.sync.dma_start(x_table[1][:], xf_rows[1])
+        nc.sync.dma_start(ra_t[:], ra[0].rearrange("(g p t) -> p g t", g=PASSES, t=PACK))
         nc.sync.dma_start(g_list[:], offs2)
-        for h in range(HALVES):
-            nc.sync.dma_start(g_table[h][:], gt[h * P : (h + 1) * P, :])
-            for g in range(PASSES):
-                nc.sync.dma_start(pred[h][g][:], pr[h * P : (h + 1) * P, g * PASS : (g + 1) * PASS])
+        nc.sync.dma_start(g_table[0][:], gt[:P, :])
+        load_predictions(0, 0)
+        nc.sync.dma_start(g_table[1][:], gt[P:, :])
+        nc.sync.dma_start(rb_t[:], rb[0].rearrange("(g p t) -> p g t", g=PASSES, t=PACK))
+        load_predictions(0, 1)
+        load_predictions(1, 0)
+        load_predictions(1, 1)
         nc.sync.dma_start(mom_t[:], mom.rearrange("(p a) n -> p a n", a=HALVES))
         nc.sync.dma_start(old_t[:], old.rearrange("(p a) n -> p a n", a=HALVES))
         make_identity(nc, ident[:])
@@ -71,13 +77,14 @@ def tile_list_moment_centred_errors_momentum_kernel(tc, xf, ra, gt, rb, pr, mom,
             nc.scalar.activation(picked[:], window(table, offsets, g), ACT.Copy)
             return picked
 
-        def group_means(groups, axis, name):
-            sums = keep.tile([P, PASS // GROUP], F32, name=name + "_sums", align_bytes=64)
-            nc.vector.tensor_reduce(sums[:], groups, axis, ALU.add)
+        def group_means(groups, axis, name, sums=None):
+            if sums is None:
+                sums = keep.tile([P, PASS // GROUP], F32, name=name + "_sums")[:]
+            nc.vector.tensor_reduce(sums, groups, axis, ALU.add)
             minus_mean = keep.tile([P, P], F32, name=name + "_minus_mean")
             nc.gpsimd.tensor_scalar(
                 minus_mean[:].rearrange("k (b e) -> k b e", e=2),
-                sums[:].unsqueeze(2).to_broadcast([P, PASS // GROUP, 2]),
+                sums.unsqueeze(2).to_broadcast([P, PASS // GROUP, 2]),
                 -1.0 / GROUP,
                 0.0,
                 ALU.mult,
@@ -85,8 +92,8 @@ def tile_list_moment_centred_errors_momentum_kernel(tc, xf, ra, gt, rb, pr, mom,
             )
             return minus_mean
 
-        def means_in_list_order(picked, name):
-            return group_means(picked[:].rearrange("k (b e) -> k b e", e=GROUP), mybir.AxisListType.X, name)
+        def means_in_list_order(picked, name, sums=None):
+            return group_means(picked[:].rearrange("k (b e) -> k b e", e=GROUP), mybir.AxisListType.X, name, sums)
 
         def turn_adding(slots, minus_mean):
             bank = turn_banks.tile([P, PACK, P], F32, name="turned")
@@ -141,41 +148,48 @@ def tile_list_moment_centred_errors_momentum_kernel(tc, xf, ra, gt, rb, pr, mom,
                 nc.tensor.transpose(bank[:, t, :], error[:, t::PACK], ident[:])
             return bank
 
-        def multiply(moment, h, g):
-            for a in range(HALVES):
-                nc.tensor.matmul_mx(
-                    moment[:, a, :],
-                    lhsT=u_q[a, g][0],
-                    lhsT_scale=u_q[a, g][1],
-                    rhs=g_q[h, g][0],
-                    rhs_scale=g_q[h, g][1],
-                    start=(g == 0 and a == 0),
-                    stop=(g == PASSES - 1 and a == HALVES - 1),
-                )
+        def multiply(moment, a, h, g, start, stop):
+            nc.tensor.matmul_mx(
+                moment,
+                lhsT=u_q[a, g][0],
+                lhsT_scale=u_q[a, g][1],
+                rhs=g_q[h, g][0],
+                rhs_scale=g_q[h, g][1],
+                start=start,
+                stop=stop,
+            )
 
         out_rows = out.rearrange("(p a) n -> p a n", a=HALVES)
 
-        def soften(h, moment, part, tag=None):
+        def step_and_root(moment, h, part):
             cols = slice(h * P, (h + 1) * P)
             shape = [P, part.stop - part.start, P]
             name = f"{h}{part.start}"
-            step = keep.tile(shape, F32, name="step" + name, tag=tag or "step" + name, align_bytes=64)
-            nc.vector.scalar_tensor_tensor(step[:], mom_t[:, part, cols], 15.0, moment[:, part, :], ALU.mult, ALU.add)
+            step = keep.tile(shape, F32, name="step" + name)
+            nc.vector.scalar_tensor_tensor(step[:], mom_t[:, part, cols], 15.0, moment, ALU.mult, ALU.add)
             size = keep.tile(shape, F32, name="size" + name)
             nc.scalar.activation(size[:], step[:], ACT.Abs, scale=0.04)
             root = keep.tile(shape, F32, name="root" + name)
             nc.scalar.activation(root[:], size[:], ACT.Abs_reciprocal_sqrt, bias=1.0)
-            damp = keep.tile(shape, F32, name="damp" + name)
-            nc.scalar.activation(damp[:], root[:], ACT.Square)
-            return step, damp
+            return step, root
 
-        def finish(h, part, step, damp):
-            cols = slice(h * P, (h + 1) * P)
-            shape = [P, part.stop - part.start, P]
-            name = f"{h}{part.start}"
-            soft = keep.tile(shape, F32, name="soft" + name)
+        def soften_on_vector(step, root, name):
+            half_soft = keep.tile(step.shape, F32, name="half_soft" + name)
+            nc.vector.scalar_tensor_tensor(half_soft[:], step[:], 0.04, root[:], ALU.mult, ALU.mult)
+            soft = keep.tile(step.shape, F32, name="soft" + name)
+            nc.vector.tensor_tensor(soft[:], half_soft[:], root[:], ALU.mult)
+            return soft
+
+        def soften_squaring_on_scalar(step, root, name):
+            damp = keep.tile(step.shape, F32, name="damp" + name)
+            nc.scalar.activation(damp[:], root[:], ACT.Square)
+            soft = keep.tile(step.shape, F32, name="soft" + name)
             nc.vector.scalar_tensor_tensor(soft[:], step[:], 0.04, damp[:], ALU.mult, ALU.mult)
-            result = keep.tile(shape, F32, name="result" + name)
+            return soft
+
+        def finish(h, part, soft):
+            cols = slice(h * P, (h + 1) * P)
+            result = keep.tile(soft.shape, F32, name=f"result{h}{part.start}")
             nc.vector.scalar_tensor_tensor(result[:], old_t[:, part, cols], 0.5, soft[:], ALU.mult, ALU.subtract)
             nc.sync.dma_start(out_rows[:, part, cols], result[:])
 
@@ -191,19 +205,22 @@ def tile_list_moment_centred_errors_momentum_kernel(tc, xf, ra, gt, rb, pr, mom,
         for h in range(HALVES):
             for g in range(PASSES):
                 g_picked[h, g] = gather(g_table[h], g_list, g, f"g_picked{h}{g}")
-        m1 = [means_in_list_order(x1[g], f"x1{g}") for g in range(PASSES)]
-        b1 = [turn_adding(stepped(x1[g]), m1[g]) for g in range(PASSES)]
-        su = staging(4, "u_staged", tag="x10_sums")
+        su = staging(4, "u_staged")
         weigh(su[:, PASS : 2 * PASS], b01, ra_t, 1)
+        m1 = [
+            means_in_list_order(x1[0], "x10", su[:, : 2 * PASS // GROUP].bitcast(F32)),
+            means_in_list_order(x1[1], "x11"),
+        ]
+        b1 = [turn_adding(stepped(x1[g]), m1[g]) for g in range(PASSES)]
         weigh(su[:, :PASS], b00, ra_t, 0)
         weigh(su[:, 2 * PASS : 3 * PASS], b1[0], ra_t, 0)
         weigh(su[:, 3 * PASS :], b1[1], ra_t, 1)
         e00 = error_turned_stepped(0, 0, nc.gpsimd)
         e01 = error_turned_stepped(0, 1, nc.gpsimd)
         u_q[0, 0], u_q[0, 1], u_q[1, 0], u_q[1, 1] = quantise(su, E4M3X4, "u")
-        e10 = error_turned_stepped(1, 0, nc.vector)
-        t0 = staging(2, "g_staged0", tag="g_picked10")
+        t0 = staging(2, "g_staged0")
         weigh(t0[:, :PASS], e00, rb_t, 0)
+        e10 = error_turned_stepped(1, 0, nc.vector)
         e11 = error_turned_stepped(1, 1, nc.vector)
         weigh(t0[:, PASS:], e01, rb_t, 1)
         t10 = staging(1, "g_staged10")
@@ -211,17 +228,21 @@ def tile_list_moment_centred_errors_momentum_kernel(tc, xf, ra, gt, rb, pr, mom,
         g_q[0, 0], g_q[0, 1] = quantise(t0, E5M2X4, "g0")
         t11 = staging(1, "g_staged11")
         weigh(t11[:], e11, rb_t, 1)
-        moments = [sum_banks.tile([P, HALVES, P], F32, name="moment") for h in range(HALVES)]
-        multiply(moments[0], 0, 0)
-        multiply(moments[0], 0, 1)
+        moment0 = sum_banks.tile([P, HALVES, P], F32, name="moment0")
+        for g in range(PASSES):
+            for a in range(HALVES):
+                multiply(moment0[:, a, :], a, 0, g, g == 0 and a == 0, g == PASSES - 1 and a == HALVES - 1)
         (g_q[1, 0],) = quantise(t10, E5M2X4, "g10")
         (g_q[1, 1],) = quantise(t11, E5M2X4, "g11")
         whole = slice(0, HALVES)
-        first = soften(0, moments[0], whole)
-        multiply(moments[1], 1, 0)
-        multiply(moments[1], 1, 1)
+        first = step_and_root(moment0[:], 0, whole)
+        moment1 = [sum_banks.tile([P, 1, P], F32, name=f"moment1{a}") for a in range(HALVES)]
+        for g in range(PASSES):
+            for a in range(HALVES):
+                multiply(moment1[a][:, 0, :], a, 1, g, g == 0, g == PASSES - 1)
         parts = [slice(a, a + 1) for a in range(HALVES)]
-        last = [soften(1, moments[1], part) for part in parts]
-        finish(0, whole, *first)
-        for part, pair in zip(parts, last):
-            finish(1, part, *pair)
+        last = [step_and_root(moment1[a][:], 1, parts[a]) for a in range(HALVES)]
+        finish(0, whole, soften_on_vector(*first, "0"))
+        softs = [soften_squaring_on_scalar(*last[a], f"1{a}") for a in range(HALVES)]
+        for a in range(HALVES):
+            finish(1, parts[a], softs[a])

from contextlib import ExitStack

import concourse.mybir as mybir
from concourse.masks import make_identity

K, J, N, T = 256, 1024, 256, 2048
FLOPS = 2 * K * J * N

F32 = mybir.dt.float32
BF16 = mybir.dt.bfloat16
U32 = mybir.dt.uint32
U16 = mybir.dt.uint16
U8 = mybir.dt.uint8
E4M3X4 = mybir.dt.float8_e4m3fn_x4
E5M2X4 = mybir.dt.float8_e5m2_x4
ALU = mybir.AluOpType
ACT = mybir.ActivationFunctionType

P = 128
PACK = 4
PASS = P * PACK
PASSES = J // PASS
GROUP = 8
LIST_COLS = PASS // 16
HALVES = 2


def tile_list_moment_centred_errors_momentum_kernel(tc, xf, ra, gt, rb, pr, mom, old, offs, offs2, out):
    nc = tc.nc
    with ExitStack() as ctx:
        lists = ctx.enter_context(tc.tile_pool(name="lists", bufs=1))
        keep = ctx.enter_context(tc.tile_pool(name="keep", bufs=1))
        turn_banks = ctx.enter_context(tc.psum_pool(name="turn_banks", bufs=5))
        sum_banks = ctx.enter_context(tc.psum_pool(name="sum_banks", bufs=1))

        x_list = lists.tile([P, J // 16], U16, name="x_list")
        g_list = lists.tile([P, J // 16], U16, name="g_list")
        x_table = [keep.tile([P, T], F32, name=f"x_table{a}") for a in range(HALVES)]
        g_table = [keep.tile([P, T], F32, name=f"g_table{h}") for h in range(HALVES)]
        pred = [[keep.tile([P, PASS], F32, name=f"pred{h}{g}") for g in range(PASSES)] for h in range(HALVES)]
        ra_t = keep.tile([P, PASSES, PACK], F32, name="ra_t")
        rb_t = keep.tile([P, PASSES, PACK], F32, name="rb_t")
        mom_t = keep.tile([P, HALVES, N], F32, name="mom_t")
        old_t = keep.tile([P, HALVES, N], F32, name="old_t")
        ident = keep.tile([P, P], F32, name="ident")

        xf_rows = xf.rearrange("(p a) t -> a p t", a=HALVES)

        def load_predictions(h, g):
            nc.sync.dma_start(pred[h][g][:], pr[h * P : (h + 1) * P, g * PASS : (g + 1) * PASS])

        nc.sync.dma_start(x_table[0][:], xf_rows[0])
        nc.sync.dma_start(x_list[:], offs)
        nc.sync.dma_start(x_table[1][:], xf_rows[1])
        nc.sync.dma_start(ra_t[:], ra[0].rearrange("(g p t) -> p g t", g=PASSES, t=PACK))
        nc.sync.dma_start(g_list[:], offs2)
        nc.sync.dma_start(g_table[0][:], gt[:P, :])
        load_predictions(0, 0)
        nc.sync.dma_start(g_table[1][:], gt[P:, :])
        nc.sync.dma_start(rb_t[:], rb[0].rearrange("(g p t) -> p g t", g=PASSES, t=PACK))
        load_predictions(0, 1)
        load_predictions(1, 0)
        load_predictions(1, 1)
        nc.sync.dma_start(mom_t[:], mom.rearrange("(p a) n -> p a n", a=HALVES))
        nc.sync.dma_start(old_t[:], old.rearrange("(p a) n -> p a n", a=HALVES))
        make_identity(nc, ident[:])
        warm_in = keep.tile([P, 1], F32, name="warm_in")
        warm_out = keep.tile([P, 1], F32, name="warm_out")
        nc.vector.memset(warm_in[:], 1.0)
        nc.scalar.activation(warm_out[:], warm_in[:], ACT.Abs_reciprocal_sqrt, bias=1.0)

        def window(table, offsets, g):
            return table[:].indirect(offsets[:, g * LIST_COLS : (g + 1) * LIST_COLS])

        def gather(table, offsets, g, name):
            picked = keep.tile([P, PASS], F32, name=name, align_bytes=64)
            nc.scalar.activation(picked[:], window(table, offsets, g), ACT.Copy)
            return picked

        def group_means(groups, axis, name, sums=None):
            if sums is None:
                sums = keep.tile([P, PASS // GROUP], F32, name=name + "_sums")[:]
            nc.vector.tensor_reduce(sums, groups, axis, ALU.add)
            minus_mean = keep.tile([P, P], F32, name=name + "_minus_mean")
            nc.gpsimd.tensor_scalar(
                minus_mean[:].rearrange("k (b e) -> k b e", e=2),
                sums.unsqueeze(2).to_broadcast([P, PASS // GROUP, 2]),
                -1.0 / GROUP,
                0.0,
                ALU.mult,
                ALU.add,
            )
            return minus_mean

        def means_in_list_order(picked, name, sums=None):
            return group_means(picked[:].rearrange("k (b e) -> k b e", e=GROUP), mybir.AxisListType.X, name, sums)

        def turn_adding(slots, minus_mean):
            bank = turn_banks.tile([P, PACK, P], F32, name="turned")
            for t in range(PACK):
                nc.tensor.matmul(bank[:, t, :], slots[t], ident[:], start=(t == 0), stop=False, is_transpose=True)
            for t in range(PACK):
                nc.tensor.matmul(
                    bank[:, t, :], minus_mean[:], ident[:], start=False, stop=(t == PACK - 1), is_transpose=True
                )
            return bank

        def stepped(picked):
            return [picked[:, t::PACK] for t in range(PACK)]

        def combine_and_turn(picked, other, op, name):
            planes = keep.tile([P, PACK, P], F32, name=name)
            nc.vector.tensor_tensor(
                planes[:].rearrange("n t p -> n p t"), picked[:].rearrange("n (p t) -> n p t", t=PACK), other, op
            )
            bank = turn_banks.tile([P, PACK, P], F32, name="turned")
            for t in range(PACK):
                nc.tensor.transpose(bank[:, t, :], planes[:, t, :], ident[:])
            return bank

        def error_turned(h, g):
            predicted = pred[h][g][:].rearrange("n (p t) -> n p t", t=PACK)
            return combine_and_turn(g_picked[h, g], predicted, ALU.subtract, f"error{h}{g}")

        def staging(passes, name, tag=None):
            return keep.tile([P, passes * PASS], BF16, name=name, tag=tag or name, align_bytes=64)

        def weigh(staged, bank, weights, g):
            nc.vector.tensor_tensor(
                staged.rearrange("p (c t) -> p c t", t=PACK),
                bank[:].rearrange("p t c -> p c t"),
                weights[:, g, :].unsqueeze(1).to_broadcast([P, P, PACK]),
                ALU.mult,
            )

        def quantise(staged, fmt, name):
            words = staged.shape[1] // PACK
            codes = keep.tile([P, words], U32, name=name + "_codes", align_bytes=64)
            scales = keep.tile([P, words], U8, name=name + "_scales", align_bytes=64)
            nc.vector.quantize_mx(codes[:].bitcast(fmt), scales[:], staged[:])
            return [(codes[:, c : c + P].bitcast(fmt), scales[:, c : c + P]) for c in range(0, words, P)]

        def error_turned_stepped(h, g, engine):
            error = keep.tile([P, PASS], F32, name=f"error{h}{g}")
            engine.tensor_tensor(error[:], g_picked[h, g][:], pred[h][g][:], ALU.subtract)
            bank = turn_banks.tile([P, PACK, P], F32, name="turned")
            for t in range(PACK):
                nc.tensor.transpose(bank[:, t, :], error[:, t::PACK], ident[:])
            return bank

        def multiply(moment, a, h, g, start, stop):
            nc.tensor.matmul_mx(
                moment,
                lhsT=u_q[a, g][0],
                lhsT_scale=u_q[a, g][1],
                rhs=g_q[h, g][0],
                rhs_scale=g_q[h, g][1],
                start=start,
                stop=stop,
            )

        out_rows = out.rearrange("(p a) n -> p a n", a=HALVES)

        def step_and_root(moment, h, part):
            cols = slice(h * P, (h + 1) * P)
            shape = [P, part.stop - part.start, P]
            name = f"{h}{part.start}"
            step = keep.tile(shape, F32, name="step" + name)
            nc.vector.scalar_tensor_tensor(step[:], mom_t[:, part, cols], 15.0, moment, ALU.mult, ALU.add)
            size = keep.tile(shape, F32, name="size" + name)
            nc.scalar.activation(size[:], step[:], ACT.Abs, scale=0.04)
            root = keep.tile(shape, F32, name="root" + name)
            nc.scalar.activation(root[:], size[:], ACT.Abs_reciprocal_sqrt, bias=1.0)
            return step, root

        def soften_on_vector(step, root, name):
            half_soft = keep.tile(step.shape, F32, name="half_soft" + name)
            nc.vector.scalar_tensor_tensor(half_soft[:], step[:], 0.04, root[:], ALU.mult, ALU.mult)
            soft = keep.tile(step.shape, F32, name="soft" + name)
            nc.vector.tensor_tensor(soft[:], half_soft[:], root[:], ALU.mult)
            return soft

        def soften_squaring_on_scalar(step, root, name):
            damp = keep.tile(step.shape, F32, name="damp" + name)
            nc.scalar.activation(damp[:], root[:], ACT.Square)
            soft = keep.tile(step.shape, F32, name="soft" + name)
            nc.vector.scalar_tensor_tensor(soft[:], step[:], 0.04, damp[:], ALU.mult, ALU.mult)
            return soft

        def finish(h, part, soft):
            cols = slice(h * P, (h + 1) * P)
            result = keep.tile(soft.shape, F32, name=f"result{h}{part.start}")
            nc.vector.scalar_tensor_tensor(result[:], old_t[:, part, cols], 0.5, soft[:], ALU.mult, ALU.subtract)
            nc.sync.dma_start(out_rows[:, part, cols], result[:])

        u_q, g_q, g_picked = {}, {}, {}
        x00 = gather(x_table[0], x_list, 0, "x_picked00")
        x01 = keep.tile([P, PACK, P], F32, name="x_picked01")
        nc.vector.tensor_copy(x01[:].rearrange("k t p -> k p t"), window(x_table[0], x_list, 1))
        m01 = group_means(x01[:].rearrange("k t (b e) -> k b t e", e=2), mybir.AxisListType.XY, "x01")
        m00 = means_in_list_order(x00, "x00")
        b01 = turn_adding([x01[:, t, :] for t in range(PACK)], m01)
        b00 = turn_adding(stepped(x00), m00)
        x1 = [gather(x_table[1], x_list, g, f"x_picked1{g}") for g in range(PASSES)]
        for h in range(HALVES):
            for g in range(PASSES):
                g_picked[h, g] = gather(g_table[h], g_list, g, f"g_picked{h}{g}")
        su = staging(4, "u_staged")
        weigh(su[:, PASS : 2 * PASS], b01, ra_t, 1)
        m1 = [
            means_in_list_order(x1[0], "x10", su[:, : 2 * PASS // GROUP].bitcast(F32)),
            means_in_list_order(x1[1], "x11"),
        ]
        b1 = [turn_adding(stepped(x1[g]), m1[g]) for g in range(PASSES)]
        weigh(su[:, :PASS], b00, ra_t, 0)
        weigh(su[:, 2 * PASS : 3 * PASS], b1[0], ra_t, 0)
        weigh(su[:, 3 * PASS :], b1[1], ra_t, 1)
        e00 = error_turned_stepped(0, 0, nc.gpsimd)
        e01 = error_turned_stepped(0, 1, nc.gpsimd)
        u_q[0, 0], u_q[0, 1], u_q[1, 0], u_q[1, 1] = quantise(su, E4M3X4, "u")
        t0 = staging(2, "g_staged0")
        weigh(t0[:, :PASS], e00, rb_t, 0)
        e10 = error_turned_stepped(1, 0, nc.vector)
        e11 = error_turned_stepped(1, 1, nc.vector)
        weigh(t0[:, PASS:], e01, rb_t, 1)
        t10 = staging(1, "g_staged10")
        weigh(t10[:], e10, rb_t, 0)
        g_q[0, 0], g_q[0, 1] = quantise(t0, E5M2X4, "g0")
        t11 = staging(1, "g_staged11")
        weigh(t11[:], e11, rb_t, 1)
        moment0 = sum_banks.tile([P, HALVES, P], F32, name="moment0")
        for g in range(PASSES):
            for a in range(HALVES):
                multiply(moment0[:, a, :], a, 0, g, g == 0 and a == 0, g == PASSES - 1 and a == HALVES - 1)
        (g_q[1, 0],) = quantise(t10, E5M2X4, "g10")
        (g_q[1, 1],) = quantise(t11, E5M2X4, "g11")
        whole = slice(0, HALVES)
        first = step_and_root(moment0[:], 0, whole)
        moment1 = [sum_banks.tile([P, 1, P], F32, name=f"moment1{a}") for a in range(HALVES)]
        for g in range(PASSES):
            for a in range(HALVES):
                multiply(moment1[a][:, 0, :], a, 1, g, g == 0, g == PASSES - 1)
        parts = [slice(a, a + 1) for a in range(HALVES)]
        last = [step_and_root(moment1[a][:], 1, parts[a]) for a in range(HALVES)]
        finish(0, whole, soften_on_vector(*first, "0"))
        softs = [soften_squaring_on_scalar(*last[a], f"1{a}") for a in range(HALVES)]
        for a in range(HALVES):
            finish(1, parts[a], softs[a])
